import numpy as np
import ml_dtypes


def mxq(x, axis, fmt="e4m3"):
    dtype, down = {"e4m3": (ml_dtypes.float8_e4m3fn, 7), "e5m2": (ml_dtypes.float8_e5m2, 14)}[fmt]
    v = np.moveaxis(np.asarray(x, np.float32).astype(ml_dtypes.bfloat16).astype(np.float64), axis, -1)
    blocks = v.reshape(v.shape[:-1] + (-1, 32))
    amax = np.abs(blocks).max(-1, keepdims=True)
    byte = np.maximum(np.where(amax > 0, np.frexp(amax)[1] - 1 + 127, 0) - down, 1)
    scale = np.exp2(byte - 127.0)
    codes = (blocks / scale).astype(np.float32).astype(dtype).astype(np.float64)
    return np.moveaxis((codes * scale).reshape(v.shape), -1, axis)


WIDE = False


def mx_kscale(k):
    if not WIDE:
        return np.ones(k)
    levels = np.array([10, -10, 5, -5, 0])
    if k % 512:
        return np.exp2(np.random.permutation(np.resize(levels, k // 32))).repeat(32)
    a = np.empty((k // 512, 16))
    for p in range(k // 512):
        a[p, :8] = np.random.permutation(np.resize(levels, 8))
        for g in range(8):
            far = levels[np.abs(levels - a[p, g]) >= 10]
            a[p, g + 8] = far[np.random.randint(len(far))]
    return np.exp2(a.ravel()).repeat(32)


BF16 = ml_dtypes.bfloat16


def bf(x):
    return np.asarray(x, np.float32).astype(BF16)


def f64(x):
    return np.asarray(x).astype(np.float64)


E2M1 = np.array([0.0, 0.5, 1.0, 1.5, 2.0, 3.0, 4.0, 6.0, -0.0, -0.5, -1.0, -1.5, -2.0, -3.0, -4.0, -6.0])


def pack_weight(w, fmt):
    k, n = w.shape
    w = f64(bf(w)).reshape(k // 32, 32, n)
    amax = np.abs(w).max(1)
    if fmt == "e4m3":
        byte = np.frexp(amax)[1] - 1 + 127 - 7
    else:
        mant, ex = np.frexp(amax / 6.0)
        byte = np.where(mant > 0.5, ex, ex - 1) + 127
    byte = np.clip(np.where(amax > 0, byte, 1), 1, 254)
    scaled = (w * np.exp2(127.0 - byte)[:, None, :]).reshape(k, n).astype(np.float32)
    by_word = np.ascontiguousarray(scaled.reshape(k // 512, 128, 4, n).transpose(0, 1, 3, 2))
    if fmt == "e4m3":
        words = by_word.astype(ml_dtypes.float8_e4m3fn).view(np.uint8)
    else:
        c = by_word.astype(ml_dtypes.float4_e2m1fn).view(np.uint8) & 0xF
        words = c[..., 0::2] | (c[..., 1::2] << 4)
    return np.ascontiguousarray(words), np.ascontiguousarray(byte.astype(np.uint8).reshape(k // 512, 16, n))


def unpack_weight(words, scales, fmt):
    g, p, n, _ = words.shape
    if fmt == "e4m3":
        vals = np.ascontiguousarray(words).view(ml_dtypes.float8_e4m3fn).astype(np.float64)
    else:
        nib = np.empty((g, p, n, 4), np.uint8)
        nib[..., 0::2] = words & 0xF
        nib[..., 1::2] = words >> 4
        vals = E2M1[nib]
    vals = vals * np.repeat(np.exp2(scales.astype(np.float64) - 127.0), 8, axis=1)[..., None]
    return vals.transpose(0, 1, 3, 2).reshape(g * 512, n)
def pack4(w):
    words, scales = pack_weight(w, "e2m1")
    return words.reshape(words.shape[0], 128, -1), scales


def unpack4(words, scales):
    return unpack_weight(words.reshape(words.shape[0], 128, -1, 2), scales, "e2m1")


M, K, C, R = 2048, 1024, 512, 512


def draw0():
    s = mx_kscale(K)
    t = mx_kscale(C)
    u = mx_kscale(M)
    gain = np.random.standard_normal((C, K)) / np.sqrt(C) / t[:, None]
    gain_words, gain_scales = pack4(gain)
    return {"bands": bf(np.random.standard_normal((M, K)) * s * u[:, None]),
            "mix": bf(np.random.standard_normal((K, C)) / np.sqrt(K) / s[:, None] * t),
            "pan": bf(np.random.standard_normal((M, C)) * t * u[:, None]),
            "radio": bf((1 + 0.1 * np.random.standard_normal(K)) / s),
            "gain_words": gain_words,
            "gain_scales": gain_scales,
            "mtf": bf(np.random.standard_normal((R, M)) / np.sqrt(M) / u)}


def core(bands, mix, pan, radio, gain_words, gain_scales, mtf):
    x = f64(bands)
    intensity = mxq(x, 1, "e4m3") @ mxq(f64(mix), 0, "e4m3")
    detail = f64(pan) - intensity
    injected = mxq(detail, 1, "e4m3") @ unpack4(gain_words, gain_scales)
    sharp = x * f64(radio) + injected
    coarse = mxq(f64(mtf), 1, "e4m3") @ mxq(detail, 0, "e4m3")
    return sharp, coarse


def e4m3fn_bytes(y):
    return np.clip(np.asarray(y, np.float64), -448.0, 448.0).astype(np.float32).astype(ml_dtypes.float8_e4m3fn).view(np.uint8)


def e4m3fn_values(b):
    return np.asarray(b, np.uint8).view(ml_dtypes.float8_e4m3fn).astype(np.float64)


def setup_inputs():
    d = draw0()
    x0 = np.asarray(d['mtf']).astype(np.float64)
    s = (np.max(np.abs(x0), axis=(0,), keepdims=True) / 448.0).astype(np.float32)
    out = {}
    for k, v in d.items():
        if k == 'mtf':
            out['mtf_bytes'] = e4m3fn_bytes(x0 / s.astype(np.float64))
            out['mtf_scale'] = s
        else:
            out[k] = v
    return out


def reference(bands, mix, pan, radio, gain_words, gain_scales, mtf_bytes, mtf_scale):
    return core(bands, mix, pan, radio, gain_words, gain_scales, e4m3fn_values(mtf_bytes) * mtf_scale.astype(np.float64))

@@ -1,0 +1,354 @@
+from contextlib import ExitStack
+
+import concourse.mybir as mybir
+from concourse.masks import make_identity
+
+M, K, C, R = 2048, 1024, 512, 512
+FLOPS = 2 * M * K * C + 2 * M * C * K + 2 * R * M * C
+BYTES = 2 * M * K + 2 * K * C + 2 * M * C + 2 * K + 128 * 2 * K + 16 * K + R * M + 4 * M + 4 * M * K + 4 * R * C
+
+F32 = mybir.dt.float32
+BF16 = mybir.dt.bfloat16
+I32 = mybir.dt.int32
+U32 = mybir.dt.uint32
+U8 = mybir.dt.uint8
+FP8 = mybir.dt.float8_e4m3fn
+FP8X4 = mybir.dt.float8_e4m3fn_x4
+FP4X4 = mybir.dt.float4_e2m1fn_x4
+MULT = mybir.AluOpType.mult
+ADD = mybir.AluOpType.add
+SUB = mybir.AluOpType.subtract
+
+P = 128
+G = M // 512
+H = K // 512
+
+
+def tile_pansharpen_detail_injection_s8_kernel(
+    tc, bands, mix, pan, radio, gain_words, gain_scales, mtf_bytes, mtf_scale, sharp, coarse
+):
+    nc = tc.nc
+    with ExitStack() as ctx:
+        const = ctx.enter_context(tc.tile_pool(name="const", bufs=1))
+        work = ctx.enter_context(tc.tile_pool(name="work", bufs=2))
+        outs = ctx.enter_context(tc.tile_pool(name="outs", bufs=4))
+        ps_t = ctx.enter_context(tc.psum_pool(name="ps_t", bufs=2))
+        ps_i = ctx.enter_context(tc.psum_pool(name="ps_i", bufs=2))
+        ps_e = ctx.enter_context(tc.psum_pool(name="ps_e", bufs=2))
+        ps_o = ctx.enter_context(tc.psum_pool(name="ps_o", bufs=2))
+
+        ident = const.tile([P, P], F32, name="ident")
+        make_identity(nc, ident[:])
+        gs = const.tile([P, K], U8, name="gs", align_bytes=64)
+        nc.gpsimd.memset(gs[:].bitcast(I32), 0)
+
+        mix_raw = const.tile([P, H, 4, C], BF16, name="mix_raw", align_bytes=64)
+        bands_sb = [const.tile([P, 4, K], BF16, name=f"bands{g}", align_bytes=64) for g in range(G)]
+        pan_sb = [const.tile([P, 4, C], BF16, name=f"pan{g}", align_bytes=64) for g in range(G)]
+        scale_bc = const.tile([P, M], F32, name="scale_bc", align_bytes=64)
+        codes_sb = [const.tile([P, M], U8, name=f"codes{r}", align_bytes=64) for r in range(4)]
+        gw = const.tile([P, 2 * K], U8, name="gw", align_bytes=64)
+        radio_bc = const.tile([P, 512], BF16, name="radio_bc", align_bytes=64)
+        radio_col = const.tile([P, 4], BF16, name="radio_col", align_bytes=64)
+
+        bands_v = bands.rearrange("(g p t) k -> g p t k", p=P, t=4)
+        pan_v = pan.rearrange("(g p t) c -> g p t c", p=P, t=4)
+        mix_v = mix.rearrange("(h p j) c -> h p j c", p=P, j=4)
+        mtf_v = mtf_bytes.rearrange("(p r) k -> r p k", r=4)
+        sharp_v = sharp.rearrange("(g p t) n -> g p t n", p=P, t=4)
+        coarse_v = coarse.rearrange("(p r) c -> r p c", r=4)
+
+        ctx.enter_context(tc.manual_schedule())
+
+        def load(dst, src):
+            nc.sync.dma_start(out=dst, in_=src)
+
+        scale_src = mtf_scale.rearrange("o k -> (o k)")
+        load(mix_raw[:, 0], mix_v[0])
+        load(mix_raw[:, 1], mix_v[1])
+        for t in range(4):
+            load(bands_sb[0][:, t], bands_v[0][:, t])
+        load(scale_bc[:], scale_src.partition_broadcast(P))
+        load(codes_sb[0][:], mtf_v[0])
+        load(pan_sb[0][:], pan_v[0])
+        load(codes_sb[1][:], mtf_v[1])
+        load(radio_bc[:], radio[0:512].partition_broadcast(P))
+        load(radio_col[:], radio[512:1024].rearrange("(p t) -> p t", t=4))
+        load(gw[:].bitcast(I32), gain_words[0].bitcast(I32))
+        for q in range(4):
+            load(gs[32 * q : 32 * q + 4, :].bitcast(I32), gain_scales[0][4 * q : 4 * q + 4, :].bitcast(I32))
+        load(bands_sb[1][:], bands_v[1])
+        load(codes_sb[2][:], mtf_v[2])
+        load(pan_sb[1][:], pan_v[1])
+        load(codes_sb[3][:], mtf_v[3])
+        for g in range(2, G):
+            load(bands_sb[g][:], bands_v[g])
+            load(pan_sb[g][:], pan_v[g])
+
+        gwp = const.tile([P, 4, 256], U8, name="gwp", align_bytes=64)
+        gsp = const.tile([P, 4, P], U8, name="gsp", align_bytes=64)
+        radio_f = const.tile([P, 4], F32, name="radio_f")
+
+        mix_c = const.tile([P, H, C], U32, name="mix_c", align_bytes=64)
+        mix_s = const.tile([P, H, C], U8, name="mix_s", align_bytes=64)
+        mix_il = [const.tile([P, C, 4], BF16, name=f"mix_il{h}", align_bytes=64) for h in range(H)]
+        mtf_il = const.tile([P, G, 512, 4], BF16, name="mtf_il", align_bytes=64)
+        mtf_il_w = mtf_il[:].rearrange("p g x j -> p (g x j)").bitcast(F32).rearrange("p (g x u) -> p g x u", g=G, u=2)
+        mtf_c = const.tile([P, G, 512], U32, name="mtf_c", align_bytes=64)
+        mtf_s = const.tile([P, G, 512], U8, name="mtf_s", align_bytes=64)
+        dy_c = const.tile([P, G, C], U32, name="dy_c", align_bytes=64)
+        dy_s = const.tile([P, G, C], U8, name="dy_s", align_bytes=64)
+
+        xT, xT_w, xc, xs, d, dx, dx_c, dx_s, prod, o, s, mtf_b = ({} for _ in range(12))
+        ib, eb = {}, {}
+
+        def open_bands(g):
+            xT[g] = work.tile([P, H, 512, 4], BF16, name="xT", align_bytes=64)
+            xT_w[g] = xT[g][:].rearrange("p h x j -> p (h x j)").bitcast(F32).rearrange("p (h x u) -> p h x u", h=H, u=2)
+            xc[g] = work.tile([P, H, 512], U32, name="xc", align_bytes=64)
+            xs[g] = work.tile([P, H, 512], U8, name="xs", align_bytes=64)
+
+        def turn_bands(g, t):
+            words = bands_sb[g][:, t].bitcast(F32)
+            xt = ps_t.tile([P, H, 2, P], F32, name="xt")
+            for h in range(H):
+                for u in range(2):
+                    nc.tensor.transpose(xt[:, h, u, :], words[:, 256 * h + u : 256 * (h + 1) : 2], ident[:])
+            nc.scalar.copy(out=xT_w[g][:, :, P * t : P * (t + 1), :], in_=xt[:].rearrange("p h u x -> p h x u"))
+
+        def quantize_bands(g, h):
+            nc.vector.quantize_mx(
+                out=xc[g][:, h].bitcast(FP8X4), scales=xs[g][:, h], in_=xT[g][:, h].rearrange("p x j -> p (x j)")
+            )
+
+        def scale_mtf(r, hh):
+            if hh == 0:
+                mtf_b[r] = work.tile([P, M], BF16, name="mtf_b", align_bytes=64)
+            cols = slice(1024 * hh, 1024 * hh + 1024)
+            nc.vector.tensor_tensor(
+                out=mtf_b[r][:, cols], in0=codes_sb[r][:, cols].bitcast(FP8), in1=scale_bc[:, cols], op=MULT
+            )
+
+        def turn_mtf(r, hh):
+            words = mtf_b[r][:].bitcast(F32)
+            xt = ps_t.tile([P, 2, 2, P], F32, name="xt")
+            for i in range(2):
+                for u in range(2):
+                    g = 2 * hh + i
+                    nc.tensor.transpose(xt[:, i, u, :], words[:, 256 * g + u : 256 * (g + 1) : 2], ident[:])
+            nc.scalar.copy(
+                out=mtf_il_w[:, 2 * hh : 2 * hh + 2, P * r : P * (r + 1), :], in_=xt[:].rearrange("p i u x -> p i x u")
+            )
+
+        def quantize_mtf(g):
+            nc.vector.quantize_mx(
+                out=mtf_c[:, g].bitcast(FP8X4), scales=mtf_s[:, g], in_=mtf_il[:, g].rearrange("p x j -> p (x j)")
+            )
+
+        def intensity(g, cb):
+            cs = slice(P * cb, P * (cb + 1))
+            if cb == 0:
+                d[g] = work.tile([P, C, 4], BF16, name="d", align_bytes=64)
+            bank = ps_i.tile([P, 4, P], F32, name="bank_i")
+            ib[cb] = bank
+            for t in range(4):
+                for h in range(H):
+                    nc.tensor.matmul_mx(
+                        out=bank[:, t, :],
+                        lhsT=xc[g][:, h, P * t : P * (t + 1)].bitcast(FP8X4),
+                        lhsT_scale=xs[g][:, h, P * t : P * (t + 1)],
+                        rhs=mix_c[:, h, cs].bitcast(FP8X4),
+                        rhs_scale=mix_s[:, h, cs],
+                        start=(h == 0),
+                        stop=(h == H - 1),
+                    )
+
+        def subtract(g, cb):
+            cs = slice(P * cb, P * (cb + 1))
+            nc.vector.tensor_tensor(
+                out=d[g][:, cs, :],
+                in0=pan_sb[g][:, :, cs].rearrange("p t c -> p c t"),
+                in1=ib[cb][:].rearrange("p t c -> p c t"),
+                op=SUB,
+            )
+
+        def turn_detail(g, u):
+            words = d[g][:].rearrange("p c t -> p (c t)").bitcast(F32)
+            if u == 0:
+                dx[g] = work.tile([P, 512, 4], BF16, name="dx", align_bytes=64)
+            xt = ps_t.tile([P, 4, P], F32, name="xt")
+            for j in range(4):
+                nc.tensor.transpose(xt[:, j, :], words[:, 2 * j + u : 1024 : 8], ident[:])
+            pairs = xt[:].rearrange("p j x -> p (j x)").bitcast(BF16)
+            nc.scalar.copy(
+                out=dx[g][:, 256 * u : 256 * (u + 1), :].rearrange("p (e x) j -> p e x j", e=2),
+                in_=pairs.rearrange("p (j x e) -> p e x j", j=4, e=2),
+            )
+
+        def quantize_dx(g):
+            dx_c[g] = work.tile([P, 512], U32, name="dx_c", align_bytes=64)
+            dx_s[g] = work.tile([P, 512], U8, name="dx_s", align_bytes=64)
+            nc.vector.quantize_mx(
+                out=dx_c[g][:].bitcast(FP8X4), scales=dx_s[g][:], in_=dx[g][:].rearrange("p x j -> p (x j)")
+            )
+
+        def quantize_dy(g):
+            nc.vector.quantize_mx(
+                out=dy_c[:, g].bitcast(FP8X4), scales=dy_s[:, g], in_=d[g][:].rearrange("p c t -> p (c t)")
+            )
+
+        def products(g):
+            prod[g] = work.tile([P, 4, 512], F32, name="prod", align_bytes=64)
+            for t in range(4):
+                nc.gpsimd.tensor_tensor(out=prod[g][:, t], in0=bands_sb[g][:, t, 0:512], in1=radio_bc[:], op=MULT)
+
+        def inject_turned(g, j):
+            if j == 0:
+                o[g] = [outs.tile([P, K], F32, name="o", align_bytes=64) for t in range(4)]
+                s[g] = [work.tile([P, 512], F32, name=f"s{i}", align_bytes=64) for i in range(4)]
+            bank = ps_e.tile([P, 512], F32, name="bank_e")
+            eb[j] = bank
+            nc.tensor.matmul_mx(
+                out=bank[:],
+                lhsT=gwp[:, j].bitcast(FP4X4),
+                lhsT_scale=gsp[:, j],
+                rhs=dx_c[g][:].bitcast(FP8X4),
+                rhs_scale=dx_s[g][:],
+                start=True,
+                stop=True,
+            )
+
+        def finish_turned(g, j):
+            nc.vector.scalar_tensor_tensor(
+                out=s[g][j][:],
+                in0=xT[g][:, 1, :, j],
+                scalar=radio_f[:, j : j + 1],
+                in1=eb[j][:],
+                op0=MULT,
+                op1=ADD,
+            )
+
+        def turn_back(g, t):
+            turned = ps_o.tile([P, 4, P], F32, name="turned")
+            for j in range(4):
+                nc.tensor.transpose(turned[:, j, :], s[g][j][:, P * t : P * (t + 1)], ident[:])
+            nc.scalar.copy(
+                out=o[g][t][:, 512:1024].rearrange("p (m j) -> p m j", j=4),
+                in_=turned[:].rearrange("p j m -> p m j"),
+            )
+            nc.sync.dma_start(out=sharp_v[g][:, t], in_=o[g][t][:])
+
+        def inject(g, t):
+            bank = ps_e.tile([P, 512], F32, name="bank_e")
+            eb[4 + t] = bank
+            nc.tensor.matmul_mx(
+                out=bank[:],
+                lhsT=dx_c[g][:, P * t : P * (t + 1)].bitcast(FP8X4),
+                lhsT_scale=dx_s[g][:, P * t : P * (t + 1)],
+                rhs=gw[:, 0:1024].bitcast(FP4X4),
+                rhs_scale=gs[:, 0:512],
+                start=True,
+                stop=True,
+            )
+
+        def finish(g, t):
+            nc.vector.tensor_tensor(out=o[g][t][:, 0:512], in0=prod[g][:, t], in1=eb[4 + t][:], op=ADD)
+
+        def coarse_rows(r):
+            bank = ps_i.tile([P, C], F32, name="bank_i")
+            for g in range(G):
+                nc.tensor.matmul_mx(
+                    out=bank[:],
+                    lhsT=mtf_c[:, g, P * r : P * (r + 1)].bitcast(FP8X4),
+                    lhsT_scale=mtf_s[:, g, P * r : P * (r + 1)],
+                    rhs=dy_c[:, g].bitcast(FP8X4),
+                    rhs_scale=dy_s[:, g],
+                    start=(g == 0),
+                    stop=(g == G - 1),
+                )
+            res = work.tile([P, C], F32, name="res", align_bytes=64)
+            nc.scalar.copy(out=res[:], in_=bank[:])
+            nc.sync.dma_start(out=coarse_v[r], in_=res[:])
+
+        def mix_interleave(h):
+            eng = nc.vector.tensor_copy if h == 0 else nc.scalar.copy
+            eng(out=mix_il[h][:], in_=mix_raw[:, h].rearrange("p j c -> p c j"))
+
+        def mix_quantize(h):
+            nc.vector.quantize_mx(
+                out=mix_c[:, h].bitcast(FP8X4), scales=mix_s[:, h], in_=mix_il[h][:].rearrange("p c j -> p (c j)")
+            )
+
+        def step(g, extra):
+            def x(k):
+                for f in extra.get(k, []):
+                    f()
+            e, n = g - 1, g + 1
+            E = 0 <= e
+            I = g < G
+            T = n < G
+            if T:
+                open_bands(n)
+            if I: intensity(g, 0)
+            if E: inject_turned(e, 0); inject_turned(e, 1)
+            if I: subtract(g, 0)
+            if E: finish_turned(e, 0); finish_turned(e, 1)
+            x(0)
+            if I: intensity(g, 1)
+            if E: inject_turned(e, 2); inject_turned(e, 3)
+            if I: subtract(g, 1)
+            if E: finish_turned(e, 2); finish_turned(e, 3)
+            x(1)
+            if T: turn_bands(n, 0); turn_bands(n, 1)
+            if I: intensity(g, 2)
+            if E: inject(e, 0); inject(e, 1)
+            if I: subtract(g, 2)
+            if E: finish(e, 0); finish(e, 1)
+            x(2)
+            if E: turn_back(e, 0); turn_back(e, 1)
+            if I: intensity(g, 3)
+            if E: inject(e, 2); inject(e, 3)
+            if I: subtract(g, 3)
+            if E: finish(e, 2); finish(e, 3)
+            x(3)
+            if T: turn_bands(n, 2); turn_bands(n, 3)
+            if I: turn_detail(g, 0); turn_detail(g, 1); quantize_dy(g)
+            if E: turn_back(e, 2); turn_back(e, 3)
+            x(4)
+            if T: quantize_bands(n, 0); quantize_bands(n, 1)
+            if I: quantize_dx(g)
+            if T: products(n)
+
+        open_bands(0)
+        mix_interleave(0)
+        mix_interleave(1)
+        for t in range(4):
+            turn_bands(0, t)
+        mix_quantize(0)
+        mix_quantize(1)
+        quantize_bands(0, 0)
+        quantize_bands(0, 1)
+        nc.gpsimd.tensor_copy(out=radio_f[:], in_=radio_col[:])
+        products(0)
+        nc.gpsimd.tensor_copy(
+            out=gwp[:].rearrange("p t (m b) -> p m t b", b=2),
+            in_=gw[:, K : 2 * K].rearrange("p (m t b) -> p m t b", t=4, b=2),
+        )
+        nc.gpsimd.tensor_copy(
+            out=gsp[:].rearrange("p t m -> p m t"), in_=gs[:, 512:1024].rearrange("p (m t) -> p m t", t=4)
+        )
+
+        def sm(r, hh):
+            return lambda: scale_mtf(r, hh)
+
+        def tm(r, hh):
+            return lambda: turn_mtf(r, hh)
+
+        def qm(g):
+            return lambda: quantize_mtf(g)
+
+        step(0, {0: [sm(0, 0), sm(0, 1)], 1: [tm(0, 0), tm(0, 1), sm(1, 0)], 2: [sm(1, 1)], 3: [tm(1, 0), tm(1, 1)], 4: [sm(2, 0)]})
+        step(1, {0: [sm(2, 1)], 2: [tm(2, 0), tm(2, 1)], 4: [sm(3, 0)]})
+        step(2, {0: [sm(3, 1)], 2: [tm(3, 0), tm(3, 1)], 4: [qm(0), qm(1)]})
+        step(3, {0: [qm(2), qm(3)]})
+        step(4, {0: [lambda: coarse_rows(0)], 1: [lambda: coarse_rows(1)], 2: [lambda: coarse_rows(2)], 3: [lambda: coarse_rows(3)]})

@@ -20,6 +20,10 @@ ADD = mybir.AluOpType.add
 SUB = mybir.AluOpType.subtract
 
 P = 128
+LOADS = """c3 m1 a3 a2 a0 a1 m0 c0 p3 s0 b0 r c2 p0 b1 c1 s1 p1 B2 g B3 p2"""
+HEAD = """w w t0 w w m1 w w m0 w t1 t2 w w t3 w b0 b1 w w w M1 v w M0 w I0 S0 w"""
+STEP = """i1 t0 t1 t2 t3 w v s1 w w w p0 v w i2 j0 q6 p1 v v j1 f0 j2 w f1 p2 v v w q7 f2 b0 p3 s2 i3 j3 s3 j4 f3 j5 v w b1 p4 d0 f4 d1 v j6 c0 c1 v w f5 v y f6 w I0 j7 p5 w v S0 f7 w x w"""
+TAIL = """w w j0 j1 j2 f0 j3 q6 v f1 j4 q7 f2 f3 j5 j6 f4 v f5 f6 v v j7 f7 v v"""
 G = M // 512
 H = K // 512
 
@@ -31,14 +35,17 @@ def tile_pansharpen_detail_injection_s8_kernel(
     with ExitStack() as ctx:
         const = ctx.enter_context(tc.tile_pool(name="const", bufs=1))
         work = ctx.enter_context(tc.tile_pool(name="work", bufs=2))
-        outs = ctx.enter_context(tc.tile_pool(name="outs", bufs=4))
-        ps_t = ctx.enter_context(tc.psum_pool(name="ps_t", bufs=2))
+        turned_pool = ctx.enter_context(tc.tile_pool(name="turned_pool", bufs=3))
+        mtf_pool = ctx.enter_context(tc.tile_pool(name="mtf_pool", bufs=4))
+        outs = ctx.enter_context(tc.tile_pool(name="outs", bufs=10))
+        ps_t = ctx.enter_context(tc.psum_pool(name="ps_t", bufs=3))
         ps_i = ctx.enter_context(tc.psum_pool(name="ps_i", bufs=2))
-        ps_e = ctx.enter_context(tc.psum_pool(name="ps_e", bufs=2))
-        ps_o = ctx.enter_context(tc.psum_pool(name="ps_o", bufs=2))
+        ps_e = ctx.enter_context(tc.psum_pool(name="ps_e", bufs=3))
 
         ident = const.tile([P, P], F32, name="ident")
         make_identity(nc, ident[:])
+        ident_b = const.tile([P, P], BF16, name="ident_b", align_bytes=64)
+        nc.gpsimd.tensor_copy(out=ident_b[:], in_=ident[:])
         gs = const.tile([P, K], U8, name="gs", align_bytes=64)
         nc.gpsimd.memset(gs[:].bitcast(I32), 0)
 
@@ -48,8 +55,7 @@ def tile_pansharpen_detail_injection_s8_kernel(
         scale_bc = const.tile([P, M], F32, name="scale_bc", align_bytes=64)
         codes_sb = [const.tile([P, M], U8, name=f"codes{r}", align_bytes=64) for r in range(4)]
         gw = const.tile([P, 2 * K], U8, name="gw", align_bytes=64)
-        radio_bc = const.tile([P, 512], BF16, name="radio_bc", align_bytes=64)
-        radio_col = const.tile([P, 4], BF16, name="radio_col", align_bytes=64)
+        radio_col = const.tile([P, H, 4], BF16, name="radio_col", align_bytes=64)
 
         bands_v = bands.rearrange("(g p t) k -> g p t k", p=P, t=4)
         pan_v = pan.rearrange("(g p t) c -> g p t c", p=P, t=4)
@@ -64,30 +70,31 @@ def tile_pansharpen_detail_injection_s8_kernel(
             nc.sync.dma_start(out=dst, in_=src)
 
         scale_src = mtf_scale.rearrange("o k -> (o k)")
-        load(mix_raw[:, 0], mix_v[0])
-        load(mix_raw[:, 1], mix_v[1])
-        for t in range(4):
-            load(bands_sb[0][:, t], bands_v[0][:, t])
-        load(scale_bc[:], scale_src.partition_broadcast(P))
-        load(codes_sb[0][:], mtf_v[0])
-        load(pan_sb[0][:], pan_v[0])
-        load(codes_sb[1][:], mtf_v[1])
-        load(radio_bc[:], radio[0:512].partition_broadcast(P))
-        load(radio_col[:], radio[512:1024].rearrange("(p t) -> p t", t=4))
-        load(gw[:].bitcast(I32), gain_words[0].bitcast(I32))
-        for q in range(4):
-            load(gs[32 * q : 32 * q + 4, :].bitcast(I32), gain_scales[0][4 * q : 4 * q + 4, :].bitcast(I32))
-        load(bands_sb[1][:], bands_v[1])
-        load(codes_sb[2][:], mtf_v[2])
-        load(pan_sb[1][:], pan_v[1])
-        load(codes_sb[3][:], mtf_v[3])
-        for g in range(2, G):
-            load(bands_sb[g][:], bands_v[g])
-            load(pan_sb[g][:], pan_v[g])
+        for tok in LOADS.split():
+            c, k = tok[0], int(tok[1:] or 0)
+            if c == "m":
+                load(mix_raw[:, k], mix_v[k])
+            if c == "a":
+                load(bands_sb[0][:, k], bands_v[0][:, k])
+            if c == "b":
+                load(bands_sb[1][:, 2 * k : 2 * k + 2], bands_v[1][:, 2 * k : 2 * k + 2])
+            if c == "r":
+                load(radio_col[:], radio.rearrange("(h p t) -> p h t", p=P, t=4))
+            if c == "p":
+                load(pan_sb[k][:], pan_v[k])
+            if c == "s":
+                load(scale_bc[:, 1024 * k : 1024 * (k + 1)], scale_src[1024 * k : 1024 * (k + 1)].partition_broadcast(P))
+            if c == "c":
+                load(codes_sb[k][:], mtf_v[k])
+            if c == "g":
+                load(gw[:].bitcast(I32), gain_words[0].bitcast(I32))
+                for q in range(4):
+                    load(gs[32 * q : 32 * q + 4, :].bitcast(I32), gain_scales[0][4 * q : 4 * q + 4, :].bitcast(I32))
+            if c == "B":
+                load(bands_sb[k][:], bands_v[k])
 
-        gwp = const.tile([P, 4, 256], U8, name="gwp", align_bytes=64)
-        gsp = const.tile([P, 4, P], U8, name="gsp", align_bytes=64)
-        radio_f = const.tile([P, 4], F32, name="radio_f")
+        radio_f = const.tile([P, H, 4], F32, name="radio_f")
+        diag = const.tile([P, H, 4, P], BF16, name="diag", align_bytes=64)
 
         mix_c = const.tile([P, H, C], U32, name="mix_c", align_bytes=64)
         mix_s = const.tile([P, H, C], U8, name="mix_s", align_bytes=64)
@@ -100,10 +107,10 @@ def tile_pansharpen_detail_injection_s8_kernel(
         dy_s = const.tile([P, G, C], U8, name="dy_s", align_bytes=64)
 
         xT, xT_w, xc, xs, d, dx, dx_c, dx_s, prod, o, s, mtf_b = ({} for _ in range(12))
-        ib, eb = {}, {}
+        ib, eb, xb = {}, {}, {}
 
         def open_bands(g):
-            xT[g] = work.tile([P, H, 512, 4], BF16, name="xT", align_bytes=64)
+            xT[g] = turned_pool.tile([P, H, 512, 4], BF16, name="xT", align_bytes=64)
             xT_w[g] = xT[g][:].rearrange("p h x j -> p (h x j)").bitcast(F32).rearrange("p (h x u) -> p h x u", h=H, u=2)
             xc[g] = work.tile([P, H, 512], U32, name="xc", align_bytes=64)
             xs[g] = work.tile([P, H, 512], U8, name="xs", align_bytes=64)
@@ -122,20 +129,18 @@ def tile_pansharpen_detail_injection_s8_kernel(
             )
 
         def scale_mtf(r, hh):
-            if hh == 0:
-                mtf_b[r] = work.tile([P, M], BF16, name="mtf_b", align_bytes=64)
+            mtf_b[r, hh] = mtf_pool.tile([P, 1024], BF16, name="mtf_b", align_bytes=64)
             cols = slice(1024 * hh, 1024 * hh + 1024)
             nc.vector.tensor_tensor(
-                out=mtf_b[r][:, cols], in0=codes_sb[r][:, cols].bitcast(FP8), in1=scale_bc[:, cols], op=MULT
+                out=mtf_b[r, hh][:], in0=codes_sb[r][:, cols].bitcast(FP8), in1=scale_bc[:, cols], op=MULT
             )
 
         def turn_mtf(r, hh):
-            words = mtf_b[r][:].bitcast(F32)
+            words = mtf_b[r, hh][:].bitcast(F32)
             xt = ps_t.tile([P, 2, 2, P], F32, name="xt")
             for i in range(2):
                 for u in range(2):
-                    g = 2 * hh + i
-                    nc.tensor.transpose(xt[:, i, u, :], words[:, 256 * g + u : 256 * (g + 1) : 2], ident[:])
+                    nc.tensor.transpose(xt[:, i, u, :], words[:, 256 * i + u : 256 * (i + 1) : 2], ident[:])
             nc.scalar.copy(
                 out=mtf_il_w[:, 2 * hh : 2 * hh + 2, P * r : P * (r + 1), :], in_=xt[:].rearrange("p i u x -> p i x u")
             )
@@ -167,19 +172,23 @@ def tile_pansharpen_detail_injection_s8_kernel(
             cs = slice(P * cb, P * (cb + 1))
             nc.vector.tensor_tensor(
                 out=d[g][:, cs, :],
-                in0=pan_sb[g][:, :, cs].rearrange("p t c -> p c t"),
+                in0=pan_sb[g][:, :, cb:C:4].rearrange("p t c -> p c t"),
                 in1=ib[cb][:].rearrange("p t c -> p c t"),
                 op=SUB,
             )
 
-        def turn_detail(g, u):
+        def turn_detail(g, k):
             words = d[g][:].rearrange("p c t -> p (c t)").bitcast(F32)
-            if u == 0:
+            if k == 0:
                 dx[g] = work.tile([P, 512, 4], BF16, name="dx", align_bytes=64)
-            xt = ps_t.tile([P, 4, P], F32, name="xt")
-            for j in range(4):
-                nc.tensor.transpose(xt[:, j, :], words[:, 2 * j + u : 1024 : 8], ident[:])
-            pairs = xt[:].rearrange("p j x -> p (j x)").bitcast(BF16)
+                xb[0] = ps_t.tile([P, 4, P], F32, name="xt")
+                xb[1] = ps_t.tile([P, 4, P], F32, name="xt")
+            for j in (2 * k, 2 * k + 1):
+                for u in range(2):
+                    nc.tensor.transpose(xb[u][:, j, :], words[:, 256 * j + u : 256 * (j + 1) : 2], ident[:])
+
+        def copy_detail(g, u):
+            pairs = xb[u][:].rearrange("p j x -> p (j x)").bitcast(BF16)
             nc.scalar.copy(
                 out=dx[g][:, 256 * u : 256 * (u + 1), :].rearrange("p (e x) j -> p e x j", e=2),
                 in_=pairs.rearrange("p (j x e) -> p e x j", j=4, e=2),
@@ -197,62 +206,37 @@ def tile_pansharpen_detail_injection_s8_kernel(
                 out=dy_c[:, g].bitcast(FP8X4), scales=dy_s[:, g], in_=d[g][:].rearrange("p c t -> p (c t)")
             )
 
-        def products(g):
-            prod[g] = work.tile([P, 4, 512], F32, name="prod", align_bytes=64)
-            for t in range(4):
-                nc.gpsimd.tensor_tensor(out=prod[g][:, t], in0=bands_sb[g][:, t, 0:512], in1=radio_bc[:], op=MULT)
-
-        def inject_turned(g, j):
-            if j == 0:
-                o[g] = [outs.tile([P, K], F32, name="o", align_bytes=64) for t in range(4)]
-                s[g] = [work.tile([P, 512], F32, name=f"s{i}", align_bytes=64) for i in range(4)]
-            bank = ps_e.tile([P, 512], F32, name="bank_e")
-            eb[j] = bank
-            nc.tensor.matmul_mx(
-                out=bank[:],
-                lhsT=gwp[:, j].bitcast(FP4X4),
-                lhsT_scale=gsp[:, j],
-                rhs=dx_c[g][:].bitcast(FP8X4),
-                rhs_scale=dx_s[g][:],
-                start=True,
-                stop=True,
-            )
-
-        def finish_turned(g, j):
-            nc.vector.scalar_tensor_tensor(
-                out=s[g][j][:],
-                in0=xT[g][:, 1, :, j],
-                scalar=radio_f[:, j : j + 1],
-                in1=eb[j][:],
-                op0=MULT,
-                op1=ADD,
-            )
-
-        def turn_back(g, t):
-            turned = ps_o.tile([P, 4, P], F32, name="turned")
+        def products(g, t, h):
+            if t == 0 and h == 0:
+                o[g] = [outs.tile([P, K], F32, name="o", align_bytes=64) for i in range(4)]
+            bank = ps_t.tile([P, 4, P], F32, name="xt")
             for j in range(4):
-                nc.tensor.transpose(turned[:, j, :], s[g][j][:, P * t : P * (t + 1)], ident[:])
+                nc.tensor.matmul(
+                    bank[:, j, :], xT[g][:, h, P * t : P * (t + 1), j], diag[:, h, j, :], start=True, stop=True
+                )
             nc.scalar.copy(
-                out=o[g][t][:, 512:1024].rearrange("p (m j) -> p m j", j=4),
-                in_=turned[:].rearrange("p j m -> p m j"),
+                out=o[g][t][:, 512 * h : 512 * (h + 1)].rearrange("p (m j) -> p m j", j=4),
+                in_=bank[:].rearrange("p j m -> p m j"),
             )
-            nc.sync.dma_start(out=sharp_v[g][:, t], in_=o[g][t][:])
 
-        def inject(g, t):
+        def inject(g, t, h):
             bank = ps_e.tile([P, 512], F32, name="bank_e")
-            eb[4 + t] = bank
+            eb[t, h] = bank
             nc.tensor.matmul_mx(
                 out=bank[:],
                 lhsT=dx_c[g][:, P * t : P * (t + 1)].bitcast(FP8X4),
                 lhsT_scale=dx_s[g][:, P * t : P * (t + 1)],
-                rhs=gw[:, 0:1024].bitcast(FP4X4),
-                rhs_scale=gs[:, 0:512],
+                rhs=gw[:, 1024 * h : 1024 * (h + 1)].bitcast(FP4X4),
+                rhs_scale=gs[:, 512 * h : 512 * (h + 1)],
                 start=True,
                 stop=True,
             )
 
-        def finish(g, t):
-            nc.vector.tensor_tensor(out=o[g][t][:, 0:512], in0=prod[g][:, t], in1=eb[4 + t][:], op=ADD)
+        def finish(g, t, h):
+            cols = slice(512 * h, 512 * (h + 1))
+            nc.vector.tensor_tensor(out=o[g][t][:, cols], in0=o[g][t][:, cols], in1=eb[t, h][:], op=ADD)
+            if h == H - 1:
+                nc.sync.dma_start(out=sharp_v[g][:, t], in_=o[g][t][:])
 
         def coarse_rows(r):
             bank = ps_i.tile([P, C], F32, name="bank_i")
@@ -267,76 +251,26 @@ def tile_pansharpen_detail_injection_s8_kernel(
                     stop=(g == G - 1),
                 )
             res = work.tile([P, C], F32, name="res", align_bytes=64)
-            nc.scalar.copy(out=res[:], in_=bank[:])
+            nc.scalar.copy(
+                out=res[:].rearrange("p (m i) -> p m i", i=4), in_=bank[:].rearrange("p (i m) -> p m i", i=4)
+            )
             nc.sync.dma_start(out=coarse_v[r], in_=res[:])
 
         def mix_interleave(h):
-            eng = nc.vector.tensor_copy if h == 0 else nc.scalar.copy
-            eng(out=mix_il[h][:], in_=mix_raw[:, h].rearrange("p j c -> p c j"))
+            eng = nc.vector.tensor_copy
+            eng(out=mix_il[h][:].rearrange("p (i m) j -> p i m j", i=4), in_=mix_raw[:, h].rearrange("p j (m i) -> p i m j", i=4))
 
         def mix_quantize(h):
             nc.vector.quantize_mx(
                 out=mix_c[:, h].bitcast(FP8X4), scales=mix_s[:, h], in_=mix_il[h][:].rearrange("p c j -> p (c j)")
             )
 
-        def step(g, extra):
-            def x(k):
-                for f in extra.get(k, []):
-                    f()
-            e, n = g - 1, g + 1
-            E = 0 <= e
-            I = g < G
-            T = n < G
-            if T:
-                open_bands(n)
-            if I: intensity(g, 0)
-            if E: inject_turned(e, 0); inject_turned(e, 1)
-            if I: subtract(g, 0)
-            if E: finish_turned(e, 0); finish_turned(e, 1)
-            x(0)
-            if I: intensity(g, 1)
-            if E: inject_turned(e, 2); inject_turned(e, 3)
-            if I: subtract(g, 1)
-            if E: finish_turned(e, 2); finish_turned(e, 3)
-            x(1)
-            if T: turn_bands(n, 0); turn_bands(n, 1)
-            if I: intensity(g, 2)
-            if E: inject(e, 0); inject(e, 1)
-            if I: subtract(g, 2)
-            if E: finish(e, 0); finish(e, 1)
-            x(2)
-            if E: turn_back(e, 0); turn_back(e, 1)
-            if I: intensity(g, 3)
-            if E: inject(e, 2); inject(e, 3)
-            if I: subtract(g, 3)
-            if E: finish(e, 2); finish(e, 3)
-            x(3)
-            if T: turn_bands(n, 2); turn_bands(n, 3)
-            if I: turn_detail(g, 0); turn_detail(g, 1); quantize_dy(g)
-            if E: turn_back(e, 2); turn_back(e, 3)
-            x(4)
-            if T: quantize_bands(n, 0); quantize_bands(n, 1)
-            if I: quantize_dx(g)
-            if T: products(n)
-
-        open_bands(0)
-        mix_interleave(0)
-        mix_interleave(1)
-        for t in range(4):
-            turn_bands(0, t)
-        mix_quantize(0)
-        mix_quantize(1)
-        quantize_bands(0, 0)
-        quantize_bands(0, 1)
         nc.gpsimd.tensor_copy(out=radio_f[:], in_=radio_col[:])
-        products(0)
-        nc.gpsimd.tensor_copy(
-            out=gwp[:].rearrange("p t (m b) -> p m t b", b=2),
-            in_=gw[:, K : 2 * K].rearrange("p (m t b) -> p m t b", t=4, b=2),
-        )
-        nc.gpsimd.tensor_copy(
-            out=gsp[:].rearrange("p t m -> p m t"), in_=gs[:, 512:1024].rearrange("p (m t) -> p m t", t=4)
-        )
+        for h in range(H):
+            for j in range(4):
+                nc.gpsimd.tensor_scalar(
+                    out=diag[:, h, j, :], in0=ident_b[:], scalar1=radio_f[:, h, j : j + 1], scalar2=0.0, op0=MULT, op1=ADD
+                )
 
         def sm(r, hh):
             return lambda: scale_mtf(r, hh)
@@ -347,8 +281,42 @@ def tile_pansharpen_detail_injection_s8_kernel(
         def qm(g):
             return lambda: quantize_mtf(g)
 
-        step(0, {0: [sm(0, 0), sm(0, 1)], 1: [tm(0, 0), tm(0, 1), sm(1, 0)], 2: [sm(1, 1)], 3: [tm(1, 0), tm(1, 1)], 4: [sm(2, 0)]})
-        step(1, {0: [sm(2, 1)], 2: [tm(2, 0), tm(2, 1)], 4: [sm(3, 0)]})
-        step(2, {0: [sm(3, 1)], 2: [tm(3, 0), tm(3, 1)], 4: [qm(0), qm(1)]})
-        step(3, {0: [qm(2), qm(3)]})
-        step(4, {0: [lambda: coarse_rows(0)], 1: [lambda: coarse_rows(1)], 2: [lambda: coarse_rows(2)], 3: [lambda: coarse_rows(3)]})
+        def cr(r):
+            return lambda: coarse_rows(r)
+
+        def step(order, g, vx, px):
+            e, n = g - 1, g + 1
+            E, I, T = 0 <= e, 0 <= g < G, n < G
+            vx, px = list(vx), list(px)
+            for tok in order.split():
+                c, k = tok[0], int(tok[1:] or 0)
+                u = (k // 2, k % 2)
+                if c == "j" and E: inject(e, u[0], u[1])
+                if c == "f" and E: finish(e, u[0], u[1])
+                if c == "i" and I: intensity(g, k)
+                if c == "s" and I: subtract(g, k)
+                if c == "I" and T: intensity(n, k)
+                if c == "S" and T: subtract(n, k)
+                if c == "t" and T:
+                    if k == 0: open_bands(n)
+                    turn_bands(n, k)
+                if c == "b" and T: quantize_bands(n, k)
+                if c == "p" and I: products(g, u[0], u[1])
+                if c == "q" and E and e < G: products(e, u[0], u[1])
+                if c == "d" and I: turn_detail(g, k)
+                if c == "c" and I: copy_detail(g, k)
+                if c == "y" and I: quantize_dy(g)
+                if c == "x" and I: quantize_dx(g)
+                if c == "m" and g == -1: mix_interleave(k)
+                if c == "M" and g == -1: mix_quantize(k)
+                if c == "v" and vx: vx.pop(0)()
+                if c == "w" and px: px.pop(0)()
+            for f in vx + px:
+                f()
+
+        step(HEAD, -1, [sm(0, 0), sm(2, 0), sm(1, 0), sm(3, 0)], [])
+        step(STEP, 0, [], [tm(0, 0)])
+        step(STEP, 1, [sm(2, 1), sm(1, 1), sm(3, 1)], [tm(1, 0), tm(3, 0), tm(2, 0), tm(2, 1)])
+        step(STEP, 2, [sm(0, 1), qm(1)], [])
+        step(STEP, 3, [qm(0), qm(3), qm(2)], [tm(0, 1), tm(1, 1), tm(3, 1)])
+        step(TAIL, 4, [], [cr(2), cr(3), cr(0), cr(1)])

@@ -17,13 +17,16 @@ FP8X4 = mybir.dt.float8_e4m3fn_x4
 FP4X4 = mybir.dt.float4_e2m1fn_x4
 MULT = mybir.AluOpType.mult
 ADD = mybir.AluOpType.add
+COPY = mybir.ActivationFunctionType.Copy
 SUB = mybir.AluOpType.subtract
 
 P = 128
-LOADS = """c3 m1 a3 a2 a0 a1 m0 c0 p3 s0 b0 r c2 p0 b1 c1 s1 p1 B2 g B3 p2"""
-HEAD = """w w t0 w w m1 w w m0 w t1 t2 w w t3 w b0 b1 w w w M1 v w M0 w I0 S0 w"""
-STEP = """i1 t0 t1 t2 t3 w v s1 w w w p0 v w i2 j0 q6 p1 v v j1 f0 j2 w f1 p2 v v w q7 f2 b0 p3 s2 i3 j3 s3 j4 f3 j5 v w b1 p4 d0 f4 d1 v j6 c0 c1 v w f5 v y f6 w I0 j7 p5 w v S0 f7 w x w"""
-TAIL = """w w j0 j1 j2 f0 j3 q6 v f1 j4 q7 f2 f3 j5 j6 f4 v f5 f6 v v j7 f7 v v"""
+LOADS = """m1 a0 s m0 a1 r p0 c0 c1 b0 p1 b1 g G p2 B2 p3 B3"""
+HEAD = """w m1 z w t0 w t1 Z1 w m0 w Z3 w Z0 t2 M0 w w t3 w Z2 w M1 b0 I0 v w w D S0"""
+STEP = """i1 j0 p0 j1 i2 j2 f0 w w s1 t0 f1 p1 s2 i3 w t1 t2 t3 f2 s3 v j3 q6 w q7 p2 w u1 v f3 p3 j4 b0 y d0 d1 f4 j5 f5 j6 j7 w c0 c1 x0 v w f6 v f7 I0 u7 p4 x1 p5 r1 u3 S0 u5 w"""
+TAIL = """j0 v v w j1 f0 f1 j2 q6 v v j3 v v f2 v w v f3 v v w q7 v v j4 f4 v j5 v f5 j6 v j7 f6 v v w f7 w v v v v v v v v v v"""
+GU = (1, 3, 5, 7)
+MIX_SCALAR = (0, 0)
 G = M // 512
 H = K // 512
 
@@ -37,7 +40,8 @@ def tile_pansharpen_detail_injection_s8_kernel(
         work = ctx.enter_context(tc.tile_pool(name="work", bufs=2))
         turned_pool = ctx.enter_context(tc.tile_pool(name="turned_pool", bufs=3))
         mtf_pool = ctx.enter_context(tc.tile_pool(name="mtf_pool", bufs=4))
-        outs = ctx.enter_context(tc.tile_pool(name="outs", bufs=10))
+        prod_pool = ctx.enter_context(tc.tile_pool(name="prod_pool", bufs=1))
+        outs = ctx.enter_context(tc.tile_pool(name="outs", bufs=8))
         ps_t = ctx.enter_context(tc.psum_pool(name="ps_t", bufs=3))
         ps_i = ctx.enter_context(tc.psum_pool(name="ps_i", bufs=2))
         ps_e = ctx.enter_context(tc.psum_pool(name="ps_e", bufs=3))
@@ -45,7 +49,11 @@ def tile_pansharpen_detail_injection_s8_kernel(
         ident = const.tile([P, P], F32, name="ident")
         make_identity(nc, ident[:])
         ident_b = const.tile([P, P], BF16, name="ident_b", align_bytes=64)
-        nc.gpsimd.tensor_copy(out=ident_b[:], in_=ident[:])
+        nc.scalar.copy(out=ident_b[:], in_=ident[:])
+        ones_b = const.tile([P, P], BF16, name="ones_b", align_bytes=64)
+        nc.gpsimd.memset(ones_b[:], 1.0)
+        sc_rows = const.tile([P, P], F32, name="sc_rows")
+        nc.gpsimd.memset(sc_rows[:], 0.0)
         gs = const.tile([P, K], U8, name="gs", align_bytes=64)
         nc.gpsimd.memset(gs[:].bitcast(I32), 0)
 
@@ -53,14 +61,14 @@ def tile_pansharpen_detail_injection_s8_kernel(
         bands_sb = [const.tile([P, 4, K], BF16, name=f"bands{g}", align_bytes=64) for g in range(G)]
         pan_sb = [const.tile([P, 4, C], BF16, name=f"pan{g}", align_bytes=64) for g in range(G)]
         scale_bc = const.tile([P, M], F32, name="scale_bc", align_bytes=64)
-        codes_sb = [const.tile([P, M], U8, name=f"codes{r}", align_bytes=64) for r in range(4)]
+        codes_sb = [const.tile([P, 2, M], U8, name=f"codes{i}", align_bytes=64) for i in range(2)]
         gw = const.tile([P, 2 * K], U8, name="gw", align_bytes=64)
         radio_col = const.tile([P, H, 4], BF16, name="radio_col", align_bytes=64)
 
         bands_v = bands.rearrange("(g p t) k -> g p t k", p=P, t=4)
         pan_v = pan.rearrange("(g p t) c -> g p t c", p=P, t=4)
         mix_v = mix.rearrange("(h p j) c -> h p j c", p=P, j=4)
-        mtf_v = mtf_bytes.rearrange("(p r) k -> r p k", r=4)
+        mtf_v = mtf_bytes.rearrange("(p i r) k -> i p r k", i=2, r=2)
         sharp_v = sharp.rearrange("(g p t) n -> g p t n", p=P, t=4)
         coarse_v = coarse.rearrange("(p r) c -> r p c", r=4)
 
@@ -69,13 +77,12 @@ def tile_pansharpen_detail_injection_s8_kernel(
         def load(dst, src):
             nc.sync.dma_start(out=dst, in_=src)
 
-        scale_src = mtf_scale.rearrange("o k -> (o k)")
         for tok in LOADS.split():
             c, k = tok[0], int(tok[1:] or 0)
             if c == "m":
                 load(mix_raw[:, k], mix_v[k])
             if c == "a":
-                load(bands_sb[0][:, k], bands_v[0][:, k])
+                load(bands_sb[0][:, 2 * k : 2 * k + 2], bands_v[0][:, 2 * k : 2 * k + 2])
             if c == "b":
                 load(bands_sb[1][:, 2 * k : 2 * k + 2], bands_v[1][:, 2 * k : 2 * k + 2])
             if c == "r":
@@ -83,11 +90,12 @@ def tile_pansharpen_detail_injection_s8_kernel(
             if c == "p":
                 load(pan_sb[k][:], pan_v[k])
             if c == "s":
-                load(scale_bc[:, 1024 * k : 1024 * (k + 1)], scale_src[1024 * k : 1024 * (k + 1)].partition_broadcast(P))
+                load(sc_rows[0:16, :], mtf_scale.rearrange("o (m n) -> (o m) n", n=P))
             if c == "c":
                 load(codes_sb[k][:], mtf_v[k])
             if c == "g":
                 load(gw[:].bitcast(I32), gain_words[0].bitcast(I32))
+            if c == "G":
                 for q in range(4):
                     load(gs[32 * q : 32 * q + 4, :].bitcast(I32), gain_scales[0][4 * q : 4 * q + 4, :].bitcast(I32))
             if c == "B":
@@ -95,6 +103,35 @@ def tile_pansharpen_detail_injection_s8_kernel(
 
         radio_f = const.tile([P, H, 4], F32, name="radio_f")
         diag = const.tile([P, H, 4, P], BF16, name="diag", align_bytes=64)
+        def diag_build():
+          nc.scalar.copy(out=radio_f[:], in_=radio_col[:])
+          for h in range(H):
+            for j in range(4):
+                nc.scalar.activation(
+                    out=diag[:, h, j, :], in_=ident_b[:], func=COPY, scale=radio_f[:, h, j : j + 1]
+                )
+        radio_bc = const.tile([P, H, P, 4], BF16, name="radio_bc", align_bytes=64)
+
+        def radio_spread(h):
+            xt = ps_t.tile([P, 4, P], F32, name="xt")
+            for j in range(4):
+                nc.tensor.matmul(xt[:, j, :], ones_b[:], diag[:, h, j, :], start=True, stop=True)
+            nc.scalar.copy(out=radio_bc[:, h], in_=xt[:].rearrange("p j m -> p m j"))
+
+        sc_T = const.tile([P, 16], F32, name="sc_T")
+
+        def scale_turn():
+            xt = ps_t.tile([P, 4, P], F32, name="xt")
+            nc.tensor.transpose(xt[:, 0, :], sc_rows[:], ident[:])
+            nc.scalar.copy(out=sc_T[:], in_=xt[:, 0, 0:16])
+
+        def scale_spread(b):
+            xt = ps_t.tile([P, 4, P], F32, name="xt")
+            for i in range(4):
+                m = 4 * b + i
+                nc.tensor.transpose(xt[:, i, :], sc_T[:, m : m + 1].to_broadcast([P, P]), ident[:])
+            nc.scalar.copy(out=scale_bc[:, 512 * b : 512 * (b + 1)], in_=xt[:].rearrange("p i x -> p (i x)"))
+
 
         mix_c = const.tile([P, H, C], U32, name="mix_c", align_bytes=64)
         mix_s = const.tile([P, H, C], U8, name="mix_s", align_bytes=64)
@@ -123,16 +160,18 @@ def tile_pansharpen_detail_injection_s8_kernel(
                     nc.tensor.transpose(xt[:, h, u, :], words[:, 256 * h + u : 256 * (h + 1) : 2], ident[:])
             nc.scalar.copy(out=xT_w[g][:, :, P * t : P * (t + 1), :], in_=xt[:].rearrange("p h u x -> p h x u"))
 
-        def quantize_bands(g, h):
+        def quantize_bands(g):
             nc.vector.quantize_mx(
-                out=xc[g][:, h].bitcast(FP8X4), scales=xs[g][:, h], in_=xT[g][:, h].rearrange("p x j -> p (x j)")
+                out=xc[g][:].rearrange("p h x -> p (h x)").bitcast(FP8X4),
+                scales=xs[g][:].rearrange("p h x -> p (h x)"),
+                in_=xT[g][:].rearrange("p h x j -> p (h x j)"),
             )
 
         def scale_mtf(r, hh):
             mtf_b[r, hh] = mtf_pool.tile([P, 1024], BF16, name="mtf_b", align_bytes=64)
             cols = slice(1024 * hh, 1024 * hh + 1024)
             nc.vector.tensor_tensor(
-                out=mtf_b[r, hh][:], in0=codes_sb[r][:, cols].bitcast(FP8), in1=scale_bc[:, cols], op=MULT
+                out=mtf_b[r, hh][:], in0=codes_sb[r // 2][:, r % 2, cols].bitcast(FP8), in1=scale_bc[:, cols], op=MULT
             )
 
         def turn_mtf(r, hh):
@@ -145,9 +184,12 @@ def tile_pansharpen_detail_injection_s8_kernel(
                 out=mtf_il_w[:, 2 * hh : 2 * hh + 2, P * r : P * (r + 1), :], in_=xt[:].rearrange("p i u x -> p i x u")
             )
 
-        def quantize_mtf(g):
+        def quantize_mtf(hh):
+            gs2 = slice(2 * hh, 2 * hh + 2)
             nc.vector.quantize_mx(
-                out=mtf_c[:, g].bitcast(FP8X4), scales=mtf_s[:, g], in_=mtf_il[:, g].rearrange("p x j -> p (x j)")
+                out=mtf_c[:, gs2].rearrange("p g x -> p (g x)").bitcast(FP8X4),
+                scales=mtf_s[:, gs2].rearrange("p g x -> p (g x)"),
+                in_=mtf_il[:, gs2].rearrange("p g x j -> p (g x j)"),
             )
 
         def intensity(g, cb):
@@ -171,21 +213,19 @@ def tile_pansharpen_detail_injection_s8_kernel(
         def subtract(g, cb):
             cs = slice(P * cb, P * (cb + 1))
             nc.vector.tensor_tensor(
-                out=d[g][:, cs, :],
-                in0=pan_sb[g][:, :, cb:C:4].rearrange("p t c -> p c t"),
-                in1=ib[cb][:].rearrange("p t c -> p c t"),
+                out=d[g][:].rearrange("p (i b m) t -> p b m t i", i=4, b=4)[:, cb],
+                in0=pan_sb[g][:, :, cs].rearrange("p t (m i) -> p m t i", i=4),
+                in1=ib[cb][:].rearrange("p t (m i) -> p m t i", i=4),
                 op=SUB,
             )
 
-        def turn_detail(g, k):
+        def turn_detail(g, u):
             words = d[g][:].rearrange("p c t -> p (c t)").bitcast(F32)
-            if k == 0:
+            if u == 0:
                 dx[g] = work.tile([P, 512, 4], BF16, name="dx", align_bytes=64)
-                xb[0] = ps_t.tile([P, 4, P], F32, name="xt")
-                xb[1] = ps_t.tile([P, 4, P], F32, name="xt")
-            for j in (2 * k, 2 * k + 1):
-                for u in range(2):
-                    nc.tensor.transpose(xb[u][:, j, :], words[:, 256 * j + u : 256 * (j + 1) : 2], ident[:])
+            xb[u] = ps_t.tile([P, 4, P], F32, name="xt")
+            for j in range(4):
+                nc.tensor.transpose(xb[u][:, j, :], words[:, 256 * j + u : 256 * (j + 1) : 2], ident[:])
 
         def copy_detail(g, u):
             pairs = xb[u][:].rearrange("p j x -> p (j x)").bitcast(BF16)
@@ -194,11 +234,15 @@ def tile_pansharpen_detail_injection_s8_kernel(
                 in_=pairs.rearrange("p (j x e) -> p e x j", j=4, e=2),
             )
 
-        def quantize_dx(g):
-            dx_c[g] = work.tile([P, 512], U32, name="dx_c", align_bytes=64)
-            dx_s[g] = work.tile([P, 512], U8, name="dx_s", align_bytes=64)
+        def quantize_dx(g, u):
+            if u == 0:
+                dx_c[g] = work.tile([P, 512], U32, name="dx_c", align_bytes=64)
+                dx_s[g] = work.tile([P, 512], U8, name="dx_s", align_bytes=64)
+            cols = slice(256 * u, 256 * (u + 1))
             nc.vector.quantize_mx(
-                out=dx_c[g][:].bitcast(FP8X4), scales=dx_s[g][:], in_=dx[g][:].rearrange("p x j -> p (x j)")
+                out=dx_c[g][:, cols].bitcast(FP8X4),
+                scales=dx_s[g][:, cols],
+                in_=dx[g][:, cols].rearrange("p x j -> p (x j)"),
             )
 
         def quantize_dy(g):
@@ -219,6 +263,15 @@ def tile_pansharpen_detail_injection_s8_kernel(
                 in_=bank[:].rearrange("p j m -> p m j"),
             )
 
+        def products_g(g, t, h):
+            prod[g, t, h] = prod_pool.tile([P, 512], F32, name=f"prod{t}{h}", align_bytes=64)
+            nc.gpsimd.tensor_tensor(
+                out=prod[g, t, h][:],
+                in0=bands_sb[g][:, t, 512 * h : 512 * (h + 1)],
+                in1=radio_bc[:, h].rearrange("p m j -> p (m j)"),
+                op=MULT,
+            )
+
         def inject(g, t, h):
             bank = ps_e.tile([P, 512], F32, name="bank_e")
             eb[t, h] = bank
@@ -234,8 +287,11 @@ def tile_pansharpen_detail_injection_s8_kernel(
 
         def finish(g, t, h):
             cols = slice(512 * h, 512 * (h + 1))
-            nc.vector.tensor_tensor(out=o[g][t][:, cols], in0=o[g][t][:, cols], in1=eb[t, h][:], op=ADD)
-            if h == H - 1:
+            first = prod[g, t, h][:] if (g, t, h) in prod else o[g][t][:, cols]
+            nc.vector.tensor_tensor(out=o[g][t][:, cols], in0=first, in1=eb[t, h][:], op=ADD)
+            if g == G - 1:
+                nc.sync.dma_start(out=sharp_v[g][:, t, cols], in_=o[g][t][:, cols])
+            elif h == H - 1:
                 nc.sync.dma_start(out=sharp_v[g][:, t], in_=o[g][t][:])
 
         def coarse_rows(r):
@@ -257,20 +313,13 @@ def tile_pansharpen_detail_injection_s8_kernel(
             nc.sync.dma_start(out=coarse_v[r], in_=res[:])
 
         def mix_interleave(h):
-            eng = nc.vector.tensor_copy
-            eng(out=mix_il[h][:].rearrange("p (i m) j -> p i m j", i=4), in_=mix_raw[:, h].rearrange("p j (m i) -> p i m j", i=4))
+            eng = (nc.vector.tensor_copy, nc.scalar.copy)[MIX_SCALAR[h]]
+            eng(out=mix_il[h][:].rearrange("p (m i) j -> p m j i", i=4), in_=mix_raw[:, h].rearrange("p j (m i) -> p m j i", i=4))
 
         def mix_quantize(h):
             nc.vector.quantize_mx(
                 out=mix_c[:, h].bitcast(FP8X4), scales=mix_s[:, h], in_=mix_il[h][:].rearrange("p c j -> p (c j)")
             )
-
-        nc.gpsimd.tensor_copy(out=radio_f[:], in_=radio_col[:])
-        for h in range(H):
-            for j in range(4):
-                nc.gpsimd.tensor_scalar(
-                    out=diag[:, h, j, :], in0=ident_b[:], scalar1=radio_f[:, h, j : j + 1], scalar2=0.0, op0=MULT, op1=ADD
-                )
 
         def sm(r, hh):
             return lambda: scale_mtf(r, hh)
@@ -300,13 +349,18 @@ def tile_pansharpen_detail_injection_s8_kernel(
                 if c == "t" and T:
                     if k == 0: open_bands(n)
                     turn_bands(n, k)
-                if c == "b" and T: quantize_bands(n, k)
-                if c == "p" and I: products(g, u[0], u[1])
-                if c == "q" and E and e < G: products(e, u[0], u[1])
+                if c == "b" and T: quantize_bands(n)
+                if c == "p" and I and (g == 0 or k not in GU): products(g, u[0], u[1])
+                if c == "u" and 0 < g < G: products_g(g, u[0], u[1])
+                if c == "z" and g == -1: scale_turn()
+                if c == "D" and g == -1: diag_build()
+                if c == "Z" and g == -1: scale_spread(k)
+                if c == "r" and g == 0: radio_spread(k)
+                if c == "q" and E and (e == 0 or k not in GU): products(e, u[0], u[1])
                 if c == "d" and I: turn_detail(g, k)
                 if c == "c" and I: copy_detail(g, k)
                 if c == "y" and I: quantize_dy(g)
-                if c == "x" and I: quantize_dx(g)
+                if c == "x" and I: quantize_dx(g, k)
                 if c == "m" and g == -1: mix_interleave(k)
                 if c == "M" and g == -1: mix_quantize(k)
                 if c == "v" and vx: vx.pop(0)()
@@ -314,9 +368,9 @@ def tile_pansharpen_detail_injection_s8_kernel(
             for f in vx + px:
                 f()
 
-        step(HEAD, -1, [sm(0, 0), sm(2, 0), sm(1, 0), sm(3, 0)], [])
-        step(STEP, 0, [], [tm(0, 0)])
-        step(STEP, 1, [sm(2, 1), sm(1, 1), sm(3, 1)], [tm(1, 0), tm(3, 0), tm(2, 0), tm(2, 1)])
-        step(STEP, 2, [sm(0, 1), qm(1)], [])
-        step(STEP, 3, [qm(0), qm(3), qm(2)], [tm(0, 1), tm(1, 1), tm(3, 1)])
-        step(TAIL, 4, [], [cr(2), cr(3), cr(0), cr(1)])
+        step(HEAD, -1, [sm(0, 0), sm(1, 0), sm(3, 0)], [])
+        step(STEP, 0, [sm(1, 1), sm(0, 1), sm(2, 0)], [tm(0, 0), tm(1, 0)])
+        step(STEP, 1, [sm(2, 1), qm(0)], [tm(3, 0), tm(2, 0), tm(0, 1)])
+        step(STEP, 2, [sm(3, 1)], [tm(1, 1)])
+        step(STEP, 3, [qm(1)], [tm(2, 1), tm(3, 1)])
+        step(TAIL, 4, [], [cr(1), cr(2), cr(3), cr(0)])

from contextlib import ExitStack

import concourse.mybir as mybir
from concourse.masks import make_identity

M, K, C, R = 2048, 1024, 512, 512
FLOPS = 2 * M * K * C + 2 * M * C * K + 2 * R * M * C
BYTES = 2 * M * K + 2 * K * C + 2 * M * C + 2 * K + 128 * 2 * K + 16 * K + R * M + 4 * M + 4 * M * K + 4 * R * C

F32 = mybir.dt.float32
BF16 = mybir.dt.bfloat16
I32 = mybir.dt.int32
U32 = mybir.dt.uint32
U8 = mybir.dt.uint8
FP8 = mybir.dt.float8_e4m3fn
FP8X4 = mybir.dt.float8_e4m3fn_x4
FP4X4 = mybir.dt.float4_e2m1fn_x4
MULT = mybir.AluOpType.mult
ADD = mybir.AluOpType.add
COPY = mybir.ActivationFunctionType.Copy
SUB = mybir.AluOpType.subtract

P = 128
LOADS = """m1 a0 s m0 a1 r p0 c0 c1 b0 p1 b1 g G p2 B2 p3 B3"""
HEAD = """w m1 z w t0 w t1 Z1 w m0 w Z3 w Z0 t2 M0 w w t3 w Z2 w M1 b0 I0 v w w D S0"""
STEP = """i1 j0 p0 j1 i2 j2 f0 w w s1 t0 f1 p1 s2 i3 w t1 t2 t3 f2 s3 v j3 q6 w q7 p2 w u1 v f3 p3 j4 b0 y d0 d1 f4 j5 f5 j6 j7 w c0 c1 x0 v w f6 v f7 I0 u7 p4 x1 p5 r1 u3 S0 u5 w"""
TAIL = """j0 v v w j1 f0 f1 j2 q6 v v j3 v v f2 v w v f3 v v w q7 v v j4 f4 v j5 v f5 j6 v j7 f6 v v w f7 w v v v v v v v v v v"""
GU = (1, 3, 5, 7)
MIX_SCALAR = (0, 0)
G = M // 512
H = K // 512


def tile_pansharpen_detail_injection_s8_kernel(
    tc, bands, mix, pan, radio, gain_words, gain_scales, mtf_bytes, mtf_scale, sharp, coarse
):
    nc = tc.nc
    with ExitStack() as ctx:
        const = ctx.enter_context(tc.tile_pool(name="const", bufs=1))
        work = ctx.enter_context(tc.tile_pool(name="work", bufs=2))
        turned_pool = ctx.enter_context(tc.tile_pool(name="turned_pool", bufs=3))
        mtf_pool = ctx.enter_context(tc.tile_pool(name="mtf_pool", bufs=4))
        prod_pool = ctx.enter_context(tc.tile_pool(name="prod_pool", bufs=1))
        outs = ctx.enter_context(tc.tile_pool(name="outs", bufs=8))
        ps_t = ctx.enter_context(tc.psum_pool(name="ps_t", bufs=3))
        ps_i = ctx.enter_context(tc.psum_pool(name="ps_i", bufs=2))
        ps_e = ctx.enter_context(tc.psum_pool(name="ps_e", bufs=3))

        ident = const.tile([P, P], F32, name="ident")
        make_identity(nc, ident[:])
        ident_b = const.tile([P, P], BF16, name="ident_b", align_bytes=64)
        nc.scalar.copy(out=ident_b[:], in_=ident[:])
        ones_b = const.tile([P, P], BF16, name="ones_b", align_bytes=64)
        nc.gpsimd.memset(ones_b[:], 1.0)
        sc_rows = const.tile([P, P], F32, name="sc_rows")
        nc.gpsimd.memset(sc_rows[:], 0.0)
        gs = const.tile([P, K], U8, name="gs", align_bytes=64)
        nc.gpsimd.memset(gs[:].bitcast(I32), 0)

        mix_raw = const.tile([P, H, 4, C], BF16, name="mix_raw", align_bytes=64)
        bands_sb = [const.tile([P, 4, K], BF16, name=f"bands{g}", align_bytes=64) for g in range(G)]
        pan_sb = [const.tile([P, 4, C], BF16, name=f"pan{g}", align_bytes=64) for g in range(G)]
        scale_bc = const.tile([P, M], F32, name="scale_bc", align_bytes=64)
        codes_sb = [const.tile([P, 2, M], U8, name=f"codes{i}", align_bytes=64) for i in range(2)]
        gw = const.tile([P, 2 * K], U8, name="gw", align_bytes=64)
        radio_col = const.tile([P, H, 4], BF16, name="radio_col", align_bytes=64)

        bands_v = bands.rearrange("(g p t) k -> g p t k", p=P, t=4)
        pan_v = pan.rearrange("(g p t) c -> g p t c", p=P, t=4)
        mix_v = mix.rearrange("(h p j) c -> h p j c", p=P, j=4)
        mtf_v = mtf_bytes.rearrange("(p i r) k -> i p r k", i=2, r=2)
        sharp_v = sharp.rearrange("(g p t) n -> g p t n", p=P, t=4)
        coarse_v = coarse.rearrange("(p r) c -> r p c", r=4)

        ctx.enter_context(tc.manual_schedule())

        def load(dst, src):
            nc.sync.dma_start(out=dst, in_=src)

        for tok in LOADS.split():
            c, k = tok[0], int(tok[1:] or 0)
            if c == "m":
                load(mix_raw[:, k], mix_v[k])
            if c == "a":
                load(bands_sb[0][:, 2 * k : 2 * k + 2], bands_v[0][:, 2 * k : 2 * k + 2])
            if c == "b":
                load(bands_sb[1][:, 2 * k : 2 * k + 2], bands_v[1][:, 2 * k : 2 * k + 2])
            if c == "r":
                load(radio_col[:], radio.rearrange("(h p t) -> p h t", p=P, t=4))
            if c == "p":
                load(pan_sb[k][:], pan_v[k])
            if c == "s":
                load(sc_rows[0:16, :], mtf_scale.rearrange("o (m n) -> (o m) n", n=P))
            if c == "c":
                load(codes_sb[k][:], mtf_v[k])
            if c == "g":
                load(gw[:].bitcast(I32), gain_words[0].bitcast(I32))
            if c == "G":
                for q in range(4):
                    load(gs[32 * q : 32 * q + 4, :].bitcast(I32), gain_scales[0][4 * q : 4 * q + 4, :].bitcast(I32))
            if c == "B":
                load(bands_sb[k][:], bands_v[k])

        radio_f = const.tile([P, H, 4], F32, name="radio_f")
        diag = const.tile([P, H, 4, P], BF16, name="diag", align_bytes=64)
        def diag_build():
          nc.scalar.copy(out=radio_f[:], in_=radio_col[:])
          for h in range(H):
            for j in range(4):
                nc.scalar.activation(
                    out=diag[:, h, j, :], in_=ident_b[:], func=COPY, scale=radio_f[:, h, j : j + 1]
                )
        radio_bc = const.tile([P, H, P, 4], BF16, name="radio_bc", align_bytes=64)

        def radio_spread(h):
            xt = ps_t.tile([P, 4, P], F32, name="xt")
            for j in range(4):
                nc.tensor.matmul(xt[:, j, :], ones_b[:], diag[:, h, j, :], start=True, stop=True)
            nc.scalar.copy(out=radio_bc[:, h], in_=xt[:].rearrange("p j m -> p m j"))

        sc_T = const.tile([P, 16], F32, name="sc_T")

        def scale_turn():
            xt = ps_t.tile([P, 4, P], F32, name="xt")
            nc.tensor.transpose(xt[:, 0, :], sc_rows[:], ident[:])
            nc.scalar.copy(out=sc_T[:], in_=xt[:, 0, 0:16])

        def scale_spread(b):
            xt = ps_t.tile([P, 4, P], F32, name="xt")
            for i in range(4):
                m = 4 * b + i
                nc.tensor.transpose(xt[:, i, :], sc_T[:, m : m + 1].to_broadcast([P, P]), ident[:])
            nc.scalar.copy(out=scale_bc[:, 512 * b : 512 * (b + 1)], in_=xt[:].rearrange("p i x -> p (i x)"))


        mix_c = const.tile([P, H, C], U32, name="mix_c", align_bytes=64)
        mix_s = const.tile([P, H, C], U8, name="mix_s", align_bytes=64)
        mix_il = [const.tile([P, C, 4], BF16, name=f"mix_il{h}", align_bytes=64) for h in range(H)]
        mtf_il = const.tile([P, G, 512, 4], BF16, name="mtf_il", align_bytes=64)
        mtf_il_w = mtf_il[:].rearrange("p g x j -> p (g x j)").bitcast(F32).rearrange("p (g x u) -> p g x u", g=G, u=2)
        mtf_c = const.tile([P, G, 512], U32, name="mtf_c", align_bytes=64)
        mtf_s = const.tile([P, G, 512], U8, name="mtf_s", align_bytes=64)
        dy_c = const.tile([P, G, C], U32, name="dy_c", align_bytes=64)
        dy_s = const.tile([P, G, C], U8, name="dy_s", align_bytes=64)

        xT, xT_w, xc, xs, d, dx, dx_c, dx_s, prod, o, s, mtf_b = ({} for _ in range(12))
        ib, eb, xb = {}, {}, {}

        def open_bands(g):
            xT[g] = turned_pool.tile([P, H, 512, 4], BF16, name="xT", align_bytes=64)
            xT_w[g] = xT[g][:].rearrange("p h x j -> p (h x j)").bitcast(F32).rearrange("p (h x u) -> p h x u", h=H, u=2)
            xc[g] = work.tile([P, H, 512], U32, name="xc", align_bytes=64)
            xs[g] = work.tile([P, H, 512], U8, name="xs", align_bytes=64)

        def turn_bands(g, t):
            words = bands_sb[g][:, t].bitcast(F32)
            xt = ps_t.tile([P, H, 2, P], F32, name="xt")
            for h in range(H):
                for u in range(2):
                    nc.tensor.transpose(xt[:, h, u, :], words[:, 256 * h + u : 256 * (h + 1) : 2], ident[:])
            nc.scalar.copy(out=xT_w[g][:, :, P * t : P * (t + 1), :], in_=xt[:].rearrange("p h u x -> p h x u"))

        def quantize_bands(g):
            nc.vector.quantize_mx(
                out=xc[g][:].rearrange("p h x -> p (h x)").bitcast(FP8X4),
                scales=xs[g][:].rearrange("p h x -> p (h x)"),
                in_=xT[g][:].rearrange("p h x j -> p (h x j)"),
            )

        def scale_mtf(r, hh):
            mtf_b[r, hh] = mtf_pool.tile([P, 1024], BF16, name="mtf_b", align_bytes=64)
            cols = slice(1024 * hh, 1024 * hh + 1024)
            nc.vector.tensor_tensor(
                out=mtf_b[r, hh][:], in0=codes_sb[r // 2][:, r % 2, cols].bitcast(FP8), in1=scale_bc[:, cols], op=MULT
            )

        def turn_mtf(r, hh):
            words = mtf_b[r, hh][:].bitcast(F32)
            xt = ps_t.tile([P, 2, 2, P], F32, name="xt")
            for i in range(2):
                for u in range(2):
                    nc.tensor.transpose(xt[:, i, u, :], words[:, 256 * i + u : 256 * (i + 1) : 2], ident[:])
            nc.scalar.copy(
                out=mtf_il_w[:, 2 * hh : 2 * hh + 2, P * r : P * (r + 1), :], in_=xt[:].rearrange("p i u x -> p i x u")
            )

        def quantize_mtf(hh):
            gs2 = slice(2 * hh, 2 * hh + 2)
            nc.vector.quantize_mx(
                out=mtf_c[:, gs2].rearrange("p g x -> p (g x)").bitcast(FP8X4),
                scales=mtf_s[:, gs2].rearrange("p g x -> p (g x)"),
                in_=mtf_il[:, gs2].rearrange("p g x j -> p (g x j)"),
            )

        def intensity(g, cb):
            cs = slice(P * cb, P * (cb + 1))
            if cb == 0:
                d[g] = work.tile([P, C, 4], BF16, name="d", align_bytes=64)
            bank = ps_i.tile([P, 4, P], F32, name="bank_i")
            ib[cb] = bank
            for t in range(4):
                for h in range(H):
                    nc.tensor.matmul_mx(
                        out=bank[:, t, :],
                        lhsT=xc[g][:, h, P * t : P * (t + 1)].bitcast(FP8X4),
                        lhsT_scale=xs[g][:, h, P * t : P * (t + 1)],
                        rhs=mix_c[:, h, cs].bitcast(FP8X4),
                        rhs_scale=mix_s[:, h, cs],
                        start=(h == 0),
                        stop=(h == H - 1),
                    )

        def subtract(g, cb):
            cs = slice(P * cb, P * (cb + 1))
            nc.vector.tensor_tensor(
                out=d[g][:].rearrange("p (i b m) t -> p b m t i", i=4, b=4)[:, cb],
                in0=pan_sb[g][:, :, cs].rearrange("p t (m i) -> p m t i", i=4),
                in1=ib[cb][:].rearrange("p t (m i) -> p m t i", i=4),
                op=SUB,
            )

        def turn_detail(g, u):
            words = d[g][:].rearrange("p c t -> p (c t)").bitcast(F32)
            if u == 0:
                dx[g] = work.tile([P, 512, 4], BF16, name="dx", align_bytes=64)
            xb[u] = ps_t.tile([P, 4, P], F32, name="xt")
            for j in range(4):
                nc.tensor.transpose(xb[u][:, j, :], words[:, 256 * j + u : 256 * (j + 1) : 2], ident[:])

        def copy_detail(g, u):
            pairs = xb[u][:].rearrange("p j x -> p (j x)").bitcast(BF16)
            nc.scalar.copy(
                out=dx[g][:, 256 * u : 256 * (u + 1), :].rearrange("p (e x) j -> p e x j", e=2),
                in_=pairs.rearrange("p (j x e) -> p e x j", j=4, e=2),
            )

        def quantize_dx(g, u):
            if u == 0:
                dx_c[g] = work.tile([P, 512], U32, name="dx_c", align_bytes=64)
                dx_s[g] = work.tile([P, 512], U8, name="dx_s", align_bytes=64)
            cols = slice(256 * u, 256 * (u + 1))
            nc.vector.quantize_mx(
                out=dx_c[g][:, cols].bitcast(FP8X4),
                scales=dx_s[g][:, cols],
                in_=dx[g][:, cols].rearrange("p x j -> p (x j)"),
            )

        def quantize_dy(g):
            nc.vector.quantize_mx(
                out=dy_c[:, g].bitcast(FP8X4), scales=dy_s[:, g], in_=d[g][:].rearrange("p c t -> p (c t)")
            )

        def products(g, t, h):
            if t == 0 and h == 0:
                o[g] = [outs.tile([P, K], F32, name="o", align_bytes=64) for i in range(4)]
            bank = ps_t.tile([P, 4, P], F32, name="xt")
            for j in range(4):
                nc.tensor.matmul(
                    bank[:, j, :], xT[g][:, h, P * t : P * (t + 1), j], diag[:, h, j, :], start=True, stop=True
                )
            nc.scalar.copy(
                out=o[g][t][:, 512 * h : 512 * (h + 1)].rearrange("p (m j) -> p m j", j=4),
                in_=bank[:].rearrange("p j m -> p m j"),
            )

        def products_g(g, t, h):
            prod[g, t, h] = prod_pool.tile([P, 512], F32, name=f"prod{t}{h}", align_bytes=64)
            nc.gpsimd.tensor_tensor(
                out=prod[g, t, h][:],
                in0=bands_sb[g][:, t, 512 * h : 512 * (h + 1)],
                in1=radio_bc[:, h].rearrange("p m j -> p (m j)"),
                op=MULT,
            )

        def inject(g, t, h):
            bank = ps_e.tile([P, 512], F32, name="bank_e")
            eb[t, h] = bank
            nc.tensor.matmul_mx(
                out=bank[:],
                lhsT=dx_c[g][:, P * t : P * (t + 1)].bitcast(FP8X4),
                lhsT_scale=dx_s[g][:, P * t : P * (t + 1)],
                rhs=gw[:, 1024 * h : 1024 * (h + 1)].bitcast(FP4X4),
                rhs_scale=gs[:, 512 * h : 512 * (h + 1)],
                start=True,
                stop=True,
            )

        def finish(g, t, h):
            cols = slice(512 * h, 512 * (h + 1))
            first = prod[g, t, h][:] if (g, t, h) in prod else o[g][t][:, cols]
            nc.vector.tensor_tensor(out=o[g][t][:, cols], in0=first, in1=eb[t, h][:], op=ADD)
            if g == G - 1:
                nc.sync.dma_start(out=sharp_v[g][:, t, cols], in_=o[g][t][:, cols])
            elif h == H - 1:
                nc.sync.dma_start(out=sharp_v[g][:, t], in_=o[g][t][:])

        def coarse_rows(r):
            bank = ps_i.tile([P, C], F32, name="bank_i")
            for g in range(G):
                nc.tensor.matmul_mx(
                    out=bank[:],
                    lhsT=mtf_c[:, g, P * r : P * (r + 1)].bitcast(FP8X4),
                    lhsT_scale=mtf_s[:, g, P * r : P * (r + 1)],
                    rhs=dy_c[:, g].bitcast(FP8X4),
                    rhs_scale=dy_s[:, g],
                    start=(g == 0),
                    stop=(g == G - 1),
                )
            res = work.tile([P, C], F32, name="res", align_bytes=64)
            nc.scalar.copy(
                out=res[:].rearrange("p (m i) -> p m i", i=4), in_=bank[:].rearrange("p (i m) -> p m i", i=4)
            )
            nc.sync.dma_start(out=coarse_v[r], in_=res[:])

        def mix_interleave(h):
            eng = (nc.vector.tensor_copy, nc.scalar.copy)[MIX_SCALAR[h]]
            eng(out=mix_il[h][:].rearrange("p (m i) j -> p m j i", i=4), in_=mix_raw[:, h].rearrange("p j (m i) -> p m j i", i=4))

        def mix_quantize(h):
            nc.vector.quantize_mx(
                out=mix_c[:, h].bitcast(FP8X4), scales=mix_s[:, h], in_=mix_il[h][:].rearrange("p c j -> p (c j)")
            )

        def sm(r, hh):
            return lambda: scale_mtf(r, hh)

        def tm(r, hh):
            return lambda: turn_mtf(r, hh)

        def qm(g):
            return lambda: quantize_mtf(g)

        def cr(r):
            return lambda: coarse_rows(r)

        def step(order, g, vx, px):
            e, n = g - 1, g + 1
            E, I, T = 0 <= e, 0 <= g < G, n < G
            vx, px = list(vx), list(px)
            for tok in order.split():
                c, k = tok[0], int(tok[1:] or 0)
                u = (k // 2, k % 2)
                if c == "j" and E: inject(e, u[0], u[1])
                if c == "f" and E: finish(e, u[0], u[1])
                if c == "i" and I: intensity(g, k)
                if c == "s" and I: subtract(g, k)
                if c == "I" and T: intensity(n, k)
                if c == "S" and T: subtract(n, k)
                if c == "t" and T:
                    if k == 0: open_bands(n)
                    turn_bands(n, k)
                if c == "b" and T: quantize_bands(n)
                if c == "p" and I and (g == 0 or k not in GU): products(g, u[0], u[1])
                if c == "u" and 0 < g < G: products_g(g, u[0], u[1])
                if c == "z" and g == -1: scale_turn()
                if c == "D" and g == -1: diag_build()
                if c == "Z" and g == -1: scale_spread(k)
                if c == "r" and g == 0: radio_spread(k)
                if c == "q" and E and (e == 0 or k not in GU): products(e, u[0], u[1])
                if c == "d" and I: turn_detail(g, k)
                if c == "c" and I: copy_detail(g, k)
                if c == "y" and I: quantize_dy(g)
                if c == "x" and I: quantize_dx(g, k)
                if c == "m" and g == -1: mix_interleave(k)
                if c == "M" and g == -1: mix_quantize(k)
                if c == "v" and vx: vx.pop(0)()
                if c == "w" and px: px.pop(0)()
            for f in vx + px:
                f()

        step(HEAD, -1, [sm(0, 0), sm(1, 0), sm(3, 0)], [])
        step(STEP, 0, [sm(1, 1), sm(0, 1), sm(2, 0)], [tm(0, 0), tm(1, 0)])
        step(STEP, 1, [sm(2, 1), qm(0)], [tm(3, 0), tm(2, 0), tm(0, 1)])
        step(STEP, 2, [sm(3, 1)], [tm(1, 1)])
        step(STEP, 3, [qm(1)], [tm(2, 1), tm(3, 1)])
        step(TAIL, 4, [], [cr(1), cr(2), cr(3), cr(0)])
